import numpy as np
import ml_dtypes


def mxq(x, axis, fmt="e4m3"):
    dtype, down = {"e4m3": (ml_dtypes.float8_e4m3fn, 7), "e5m2": (ml_dtypes.float8_e5m2, 14)}[fmt]
    v = np.moveaxis(np.asarray(x, np.float32).astype(ml_dtypes.bfloat16).astype(np.float64), axis, -1)
    blocks = v.reshape(v.shape[:-1] + (-1, 32))
    amax = np.abs(blocks).max(-1, keepdims=True)
    byte = np.maximum(np.where(amax > 0, np.frexp(amax)[1] - 1 + 127, 0) - down, 1)
    scale = np.exp2(byte - 127.0)
    codes = (blocks / scale).astype(np.float32).astype(dtype).astype(np.float64)
    return np.moveaxis((codes * scale).reshape(v.shape), -1, axis)


WIDE = False


def mx_kscale(k):
    if not WIDE:
        return np.ones(k)
    levels = np.array([10, -10, 5, -5, 0])
    if k % 512:
        return np.exp2(np.random.permutation(np.resize(levels, k // 32))).repeat(32)
    a = np.empty((k // 512, 16))
    for p in range(k // 512):
        a[p, :8] = np.random.permutation(np.resize(levels, 8))
        for g in range(8):
            far = levels[np.abs(levels - a[p, g]) >= 10]
            a[p, g + 8] = far[np.random.randint(len(far))]
    return np.exp2(a.ravel()).repeat(32)


def f64(x):
    return np.asarray(x).astype(np.float64)


def striped(idx):
    return np.tile(idx.reshape(-1, 16).T, (8, 1)).astype(np.uint16)


def unstriped(offs):
    return offs[:16].T.reshape(-1).astype(np.int64)


E2M1 = np.array([0.0, 0.5, 1.0, 1.5, 2.0, 3.0, 4.0, 6.0, -0.0, -0.5, -1.0, -1.5, -2.0, -3.0, -4.0, -6.0])


def pack_weight(w, fmt):
    k, n = w.shape
    w = f64(np.asarray(w, np.float32).astype(ml_dtypes.bfloat16)).reshape(k // 32, 32, n)
    amax = np.abs(w).max(1)
    if fmt == "e4m3":
        byte = np.frexp(amax)[1] - 1 + 127 - 7
    else:
        mant, ex = np.frexp(amax / 6.0)
        byte = np.where(mant > 0.5, ex, ex - 1) + 127
    byte = np.clip(np.where(amax > 0, byte, 1), 1, 254)
    scaled = (w * np.exp2(127.0 - byte)[:, None, :]).reshape(k, n).astype(np.float32)
    by_word = np.ascontiguousarray(scaled.reshape(k // 512, 128, 4, n).transpose(0, 1, 3, 2))
    if fmt == "e4m3":
        words = by_word.astype(ml_dtypes.float8_e4m3fn).view(np.uint8)
    else:
        c = by_word.astype(ml_dtypes.float4_e2m1fn).view(np.uint8) & 0xF
        words = (c[..., 0::2] | (c[..., 1::2] << 4)).reshape(k // 512, 128, 2 * n)
    return np.ascontiguousarray(words), np.ascontiguousarray(byte.astype(np.uint8).reshape(k // 512, 16, n))


def unpack_weight(words, scales, fmt):
    g, _, n = scales.shape
    words = np.ascontiguousarray(words).reshape(g, 128, n, -1)
    if fmt == "e4m3":
        vals = words.view(ml_dtypes.float8_e4m3fn).astype(np.float64)
    else:
        nib = np.empty((g, 128, n, 4), np.uint8)
        nib[..., 0::2] = words & 0xF
        nib[..., 1::2] = words >> 4
        vals = E2M1[nib]
    vals = vals * np.repeat(np.exp2(scales.astype(np.float64) - 127.0), 8, axis=1)[..., None]
    return vals.transpose(0, 1, 3, 2).reshape(g * 512, n)


def gelu(v):
    return 0.5 * v * (1.0 + np.tanh(np.sqrt(2.0 / np.pi) * (v + 0.044715 * v**3)))


def striped8(idx):
    return np.concatenate([v.reshape(-1, 16).T for v in idx]).astype(np.uint16)


def unstriped8(offs):
    return np.stack([offs[16 * g:16 * g + 16].T.reshape(-1) for g in range(8)]).astype(np.int64)


def heads(h, wgt, idx8):
    r = np.arange(h.shape[0])
    return wgt[r // 4 % 128] * h[r[:, None], idx8[r % 512 // 64]]


K, T, S, H, T2, P, N = 1024, 4096, 1024, 1024, 2048, 1024, 512

def setup_inputs():
    n = np.random.standard_normal
    s = mx_kscale(K)[:, None]
    u = mx_kscale(H)[:, None]
    tab_words, tab_scales = pack_weight(n((K, T)) * s, "e4m3")
    w4_words, w4_scales = pack_weight(0.7 * n((H, N)) / np.sqrt(H) / u, "e2m1")
    strips = np.stack([np.random.permutation(T2)[:P] for _ in range(8)])
    return {
        "tab_words": tab_words, "tab_scales": tab_scales,
        "offs": striped(np.random.permutation(T)[:S]),
        "w1": (0.55 * n((K, H)) / np.sqrt(K) / s).astype(np.float32),
        "gain": (np.random.uniform(1.5, 2.5, H) * u[:, 0]).astype(np.float32),
        "page0": (n((H, T2)) * u).astype(np.float32),
        "wgs": np.exp(0.3 * n((128, S))).astype(np.float32),
        "offs2": striped(np.random.permutation(T2)[:S]),
        "wgt": np.repeat(np.random.uniform(0.5, 2.0, (8, P)), 16, axis=0).astype(np.float32),
        "offs3": striped8(strips),
        "w4_words": w4_words, "w4_scales": w4_scales,
        "w2": (n((H, N)) / np.sqrt(H) / u).astype(np.float32),
        "b2": (0.6 * n(N)).astype(np.float32),
    }

def reference(tab_words, tab_scales, offs, w1, gain, page0, wgs, offs2, wgt, offs3, w4_words, w4_scales, w2, b2):
    v = unpack_weight(tab_words, tab_scales, "e4m3")[:, unstriped(offs)]
    w4 = unpack_weight(w4_words, w4_scales, "e2m1")
    h = f64(gain)[:, None] * np.sin(mxq(f64(w1), 0, "e4m3").T @ v)
    page = f64(page0).copy()
    page[:, unstriped(offs2)] = np.tile(f64(wgs), (H // 128, 1)) * h
    x = mxq(heads(page, f64(wgt), unstriped8(offs3)), 0, "e4m3")
    base = w4.T @ x
    bend = np.tanh((mxq(f64(w2), 0, "e4m3").T @ x) + f64(b2)[:, None])
    return base + bend

@@ -1,0 +1,353 @@
+import math
+from contextlib import ExitStack
+
+import concourse.mybir as mybir
+from concourse.masks import make_identity
+
+K, T, S, H, T2, M, N = 1024, 4096, 1024, 1024, 2048, 1024, 512
+FLOPS = 2 * K * H * S + 2 * 2 * H * N * M
+
+F32 = mybir.dt.float32
+BF16 = mybir.dt.bfloat16
+I32 = mybir.dt.int32
+U32 = mybir.dt.uint32
+U16 = mybir.dt.uint16
+U8 = mybir.dt.uint8
+FP8X4 = mybir.dt.float8_e4m3fn_x4
+FP4X4 = mybir.dt.float4_e2m1fn_x4
+ACT = mybir.ActivationFunctionType
+MULT = mybir.AluOpType.mult
+ADD = mybir.AluOpType.add
+
+P = 128
+PACK = 4
+K_PASS = P * PACK
+BANK = 512
+SLICES = H // P
+TWO_PI = 2.0 * math.pi
+MAGIC = 98304.0
+MAGIC_BITS = float(0x47C00000)
+BITS_PER_TURN = 128.0
+CHUNKS = (128, 256, 256, 256, 128)
+HELD = (3, 4)
+FIRST_UNITS = (256, 256, 512)
+UNITS = (512, 512)
+LAG = 1
+PER_BANK = (4, 2, 2, 2, 2)
+
+
+def tile_list_floor_suction_reading_kernel(
+    tc, tab_words, tab_scales, offs, w1, gain, page0, wgs, offs2, wgt, offs3, w4_words, w4_scales, w2, b2, out
+):
+    nc = tc.nc
+    with ExitStack() as ctx:
+        keep = ctx.enter_context(tc.tile_pool(name="keep", bufs=1))
+        work = ctx.enter_context(tc.tile_pool(name="work", bufs=2))
+        shared = ctx.enter_context(tc.tile_pool(name="shared", bufs=1))
+        psum = ctx.enter_context(tc.psum_pool(name="psum", bufs=1))
+
+        def bank(i):
+            return psum.tile([P, BANK], F32, name="bank%d" % i)
+
+        idx1 = keep.tile([P, S // 16], U16, name="idx1")
+        idx2 = keep.tile([P, S // 16], U16, name="idx2")
+        idx3 = keep.tile([P, M // 16], U16, name="idx3")
+
+        tab_s = keep.tile([P, T], U8, name="tab_s", tag="v_w1", align_bytes=64)
+        nc.vector.memset(tab_s[:].bitcast(I32), 0)
+        nc.sync.dma_start(idx1[:], offs)
+        tab_w = []
+        for a in range(2):
+            t_ = shared.tile([P, T], I32, name="tab_w%d" % a, align_bytes=64, offset=4 * T * a)
+            nc.sync.dma_start(t_[:], tab_words[a].rearrange("p t i -> p (t i)").bitcast(I32))
+            tab_w.append(t_)
+        for q in range(4):
+            nc.gpsimd.dma_start(
+                tab_s[32 * q : 32 * q + 8, :].bitcast(I32), tab_scales[:, 4 * q : 4 * q + 4, :].bitcast(I32)
+            )
+
+        def load_w1(a, b):
+            raw = work.tile([P, PACK, K_PASS], F32, name="w1_raw", tag="w1_raw", bufs=3)
+            rows = w1[a * K_PASS : (a + 1) * K_PASS, b * K_PASS : (b + 1) * K_PASS]
+            nc.sync.dma_start(raw[:], rows.rearrange("(p i) c -> p i c", i=PACK))
+            return raw
+
+        page_rows = page0.rearrange("(b p t) c -> b t p c", b=2, t=PACK)
+
+        def load_page(s):
+            pg = work.tile([P, T2], F32, name="page", bufs=5)
+            nc.sync.dma_start(pg[:], page_rows[s // PACK, s % PACK])
+            return pg
+
+        w1_raw = {}
+        pages = {}
+        w1_raw[0, 0] = load_w1(0, 0)
+        w1_raw[1, 0] = load_w1(1, 0)
+        gains = keep.tile([P, 2, PACK], F32, name="gains")
+        nc.sync.dma_start(gains[:], gain.rearrange("(b p t) -> p b t", b=2, t=PACK))
+        wgs_rows = wgs.rearrange("(p t) j -> p t j", t=PACK)
+        wgs_first = keep.tile([P, S], F32, name="wgs_first", tag="wgs_first", align_bytes=64)
+        wgs_rest = keep.tile([P, PACK - 1, S], F32, name="wgs_rest", tag="wgs_rest", align_bytes=64)
+        for q in (0, 2, 1, 3):
+            nc.sync.dma_start(wgs_first[32 * q : 32 * q + 32, :], wgs_rows[:, 0, :])
+        nc.sync.dma_start(idx2[:], offs2)
+        pages[0] = load_page(0)
+        wgt_sb = keep.tile([P, M], F32, name="wgt_sb")
+        nc.sync.dma_start(wgt_sb[:], wgt)
+        nc.sync.dma_start(idx3[:], offs3)
+        for q in (0, 2, 1, 3):
+            nc.sync.dma_start(wgs_rest[32 * q : 32 * q + 32, :, :], wgs_rows[:, 1:, :])
+        pages[1] = load_page(1)
+        pages[2] = load_page(2)
+        w1_raw[0, 1] = load_w1(0, 1)
+        w1_raw[1, 1] = load_w1(1, 1)
+
+        ident = keep.tile([P, P], F32, name="ident")
+        make_identity(nc, ident[:])
+        neg_magic = keep.tile([P, P], F32, name="neg_magic")
+        nc.gpsimd.memset(neg_magic[:], -MAGIC)
+
+        v_w = [keep.tile([P, S], U32, name="v_w", tag="v_w%d" % a, align_bytes=64) for a in range(2)]
+        v_s = keep.tile([P, S], U8, name="v_s", align_bytes=64)
+        nc.vector.tensor_copy(v_w[0][:], tab_w[0][:].bitcast(U32).indirect(idx1[:]))
+        nc.vector.tensor_copy(v_s[:], tab_s[:].indirect(idx1[:]))
+        nc.vector.tensor_copy(v_w[1][:], tab_w[1][:].bitcast(U32).indirect(idx1[:]))
+
+        w1_c = {}
+        w1_s = {}
+        w1_bf = {}
+
+        first_bf = shared.tile([P, 4, 2, P, PACK], BF16, name="first_bf", align_bytes=64, offset=4 * T)
+
+        def cast_w1(a, b, u):
+            if b == 0:
+                bf = first_bf[:, 2 * a + u]
+            else:
+                bf = work.tile([P, 2, P, PACK], BF16, name="w_bf", tag="w_bf", bufs=4, align_bytes=64)[:]
+            src = w1_raw[a, b][:].rearrange("p i (q t) -> p q i t", t=PACK)[:, :, :, 2 * u : 2 * u + 2]
+            dst = bf.rearrange("p t q i -> p q i t")
+            if b == 0:
+                nc.vector.tensor_copy(dst, src)
+            else:
+                nc.scalar.copy(dst, src)
+            w1_bf[a, b, u] = bf
+
+        def quant_w1(a, b, u):
+            c_ = keep.tile([P, 2 * P], U32, name="w1_c", tag="w1_c%d%d%d" % (a, b, u), align_bytes=64)
+            s_ = keep.tile([P, 2 * P], U8, name="w1_s", tag="w1_s%d%d%d" % (a, b, u), align_bytes=64)
+            nc.vector.quantize_mx(
+                out=c_[:].bitcast(FP8X4), scales=s_[:], in_=w1_bf[a, b, u].rearrange("p t q i -> p (t q i)")
+            )
+            w1_c[a, b, u] = c_
+            w1_s[a, b, u] = s_
+
+        for u in range(2):
+            for a in range(2):
+                cast_w1(a, 0, u)
+                quant_w1(a, 0, u)
+        gained = shared.tile([P, S], F32, name="gained", align_bytes=64, offset=6 * T)
+        nc.vector.tensor_scalar(gained[:], wgs_first[:], gains[:, 0, 0:1], None, MULT)
+
+        def sine_unit(s, n, j0, width, sin_t):
+            b, t = divmod(s, PACK)
+            u, e = divmod(t, 2)
+            cols = slice(e * P, (e + 1) * P)
+            tiles = width // P
+            z = bank(n % 2)
+            for a in range(2):
+                for jt in range(tiles):
+                    js = slice(j0 + jt * P, j0 + (jt + 1) * P)
+                    nc.tensor.matmul_mx(
+                        out=z[:, jt * P : (jt + 1) * P],
+                        lhsT=v_w[a][:, js].bitcast(FP8X4),
+                        lhsT_scale=v_s[4 * a :, js],
+                        rhs=w1_c[a, b, u][:, cols].bitcast(FP8X4),
+                        rhs_scale=w1_s[a, b, u][:, cols],
+                        start=(a == 0 and jt == 0),
+                        stop=(a == 1 and jt == tiles - 1),
+                    )
+            whole = work.tile([P, BANK], U32, name="whole")
+            turns = work.tile([P, BANK], F32, name="turns")
+            nc.scalar.activation(
+                whole[:, :width], z[:, :width], ACT.Copy, bias=MAGIC_BITS, scale=-BITS_PER_TURN / TWO_PI
+            )
+            nc.scalar.activation(turns[:, :width], z[:, :width], ACT.Copy, scale=1.0 / TWO_PI)
+            r = bank(2 + n % 2)
+            for term in range(3):
+                for jt in range(tiles):
+                    js = slice(jt * P, (jt + 1) * P)
+                    src = (neg_magic[:], whole[:, js].bitcast(F32), turns[:, js])[term]
+                    nc.tensor.matmul(
+                        r[:, js], src, ident[:], is_transpose=True,
+                        start=(term == 0 and jt == 0), stop=(term == 2 and jt == tiles - 1),
+                    )
+            part = sin_t[:, j0 : j0 + width]
+            nc.scalar.activation(part, r[:, :width], ACT.Sin, scale=TWO_PI)
+            if s > 0:
+                nc.scalar.activation(part, part, ACT.Copy, scale=gains[:, b, t : t + 1])
+
+        starts = [sum(CHUNKS[:c]) for c in range(len(CHUNKS))]
+        picked0 = []
+        picked1 = {
+            c: keep.tile([P, PACK, w], F32, name="picked1_%d" % c) for c, w in enumerate(CHUNKS) if c not in HELD
+        }
+
+        def gather(s, dst, m0, w):
+            lists = idx3[:, m0 // 16 : (m0 + w) // 16]
+            nc.vector.tensor_tensor(dst, pages[s][:].indirect(lists), wgt_sb[:, m0 : m0 + w], MULT)
+
+        def gather_early(s):
+            b, t = divmod(s, PACK)
+            if b == 0:
+                if t == 0:
+                    picked0.append(shared.tile([P, PACK, M], F32, name="picked0", align_bytes=64, offset=4 * T))
+                gather(s, picked0[0][:, t, :], 0, M)
+            else:
+                for c, w in enumerate(CHUNKS):
+                    if c not in HELD:
+                        gather(s, picked1[c][:, t, :], starts[c], w)
+
+        def interleave(src, w, pool, tag, bufs):
+            bf = pool.tile([P, w, PACK], BF16, name="x_bf", tag=tag, bufs=bufs, align_bytes=64)
+            nc.scalar.copy(
+                bf[:].rearrange("p (c i) t -> p c t i", i=4), src.rearrange("p t (c i) -> p c t i", i=4)
+            )
+            return bf
+
+        def quantize(bf, codes, scales):
+            nc.vector.quantize_mx(out=codes.bitcast(FP8X4), scales=scales, in_=bf[:].rearrange("p c t -> p (c t)"))
+
+        x_c = {1: keep.tile([P, M], U32, name="x_c1", align_bytes=64)}
+        x_s = [keep.tile([P, M], U8, name="x_s%d" % b, align_bytes=64) for b in range(2)]
+        w2_bf = []
+        w2_s = keep.tile([P, 2, N], U8, name="w2_s", align_bytes=64)
+        w4_c = keep.tile([P, 2, 2 * N], U8, name="w4_c", align_bytes=64)
+        w4_s = keep.tile([P, 2, N], U8, name="w4_s", align_bytes=64)
+        bias = keep.tile([P, PACK], F32, name="bias")
+        w2_raw = []
+
+        def load_second():
+            raw = shared.tile([P, 2, PACK, N], F32, name="w2_raw", align_bytes=64, offset=0)
+            for b in range(2):
+                nc.sync.dma_start(
+                    raw[:, b], w2[b * K_PASS : (b + 1) * K_PASS, :].rearrange("(p i) n -> p i n", i=PACK)
+                )
+            w2_raw.append(raw)
+            nc.sync.dma_start(w4_c[:].bitcast(I32), w4_words.rearrange("b p n -> p b n").bitcast(I32))
+            nc.gpsimd.memset(w4_s[:].bitcast(I32), 0)
+            for q in range(4):
+                nc.sync.dma_start(
+                    w4_s[32 * q : 32 * q + 4].bitcast(I32),
+                    w4_scales[:, 4 * q : 4 * q + 4, :].rearrange("b r n -> r b n").bitcast(I32),
+                )
+            with nc.allow_non_contiguous_dma(reason="one bias value a partition"):
+                nc.sync.dma_start(bias[:], b2.rearrange("(g p) -> p g", p=P))
+
+        def quant_w2(b):
+            for h in range(2):
+                cols = slice(h * 256, (h + 1) * 256)
+                w2_bf.append(interleave(w2_raw[0][:, b, :, cols], 256, work, "w2_bf", 4))
+
+        def quant_x0(h):
+            for c in (2 * h, 2 * h + 1):
+                cols = slice(c * 256, (c + 1) * 256)
+                bf = interleave(picked0[0][:, :, cols], 256, keep, ("w1_c010", "w1_c110", "w1_s010", "w1_s110")[c], 1)
+                quantize(bf, x_c[0][:, cols], x_s[0][:, cols])
+
+        load_second()
+        pages[3] = load_page(3)
+        pages[4] = load_page(4)
+
+        unit = 0
+        for s in range(SLICES):
+            b, t = divmod(s, PACK)
+            sin_t = keep.tile([P, S], F32, name="sin_t", tag="sin%d" % (s % 3), align_bytes=64)
+            gw = gained[:] if s == 0 else wgs_first[:] if t == 0 else wgs_rest[:, t - 1, :]
+            widths = FIRST_UNITS if s == 0 else UNITS
+            for n, width in enumerate(widths):
+                sine_unit(s, unit, sum(widths[:n]), width, sin_t)
+                unit = unit + 1
+            if s == 0:
+                for n, width in enumerate(widths):
+                    j0 = sum(widths[:n])
+                    js = slice(j0, j0 + width)
+                    lists = idx2[:, j0 // 16 : (j0 + width) // 16]
+                    nc.vector.tensor_tensor(pages[s][:].indirect(lists), sin_t[:, js], gw[:, js], MULT)
+            else:
+                nc.vector.tensor_tensor(pages[s][:].indirect(idx2[:]), sin_t[:], gw, MULT)
+                gather_early(s - 1)
+            if 1 <= s <= 3:
+                pages[s + 4] = load_page(s + 4)
+            if s in (1, 2):
+                for a in range(2):
+                    cast_w1(a, 1, s - 1)
+                for a in range(2):
+                    quant_w1(a, 1, s - 1)
+            if s in (3, 4):
+                quant_w2(s - 3)
+            if s == 4:
+                w2_c = keep.tile([P, 2, N], U32, name="w2_c", tag="wgs_first", align_bytes=64)
+                for n, bf in enumerate(w2_bf):
+                    cols = slice(n % 2 * 256, (n % 2 + 1) * 256)
+                    quantize(bf, w2_c[:, n // 2, cols], w2_s[:, n // 2, cols])
+            if s == 5:
+                x_c[0] = keep.tile([P, M], U32, name="x_c0", tag="sin2", align_bytes=64)
+                quant_x0(0)
+                quant_x0(1)
+
+        out_rows = out.rearrange("(g p) m -> p g m", p=P)
+        held_tags = {HELD[0]: "sin1", HELD[1]: "wgs_rest"}
+
+        def finish_x(c):
+            w = CHUNKS[c]
+            cols = slice(starts[c], starts[c] + w)
+            if c in HELD:
+                picked1[c] = keep.tile([P, PACK, w], F32, name="picked1", tag=held_tags[c], align_bytes=64)
+            for t in range(0 if c in HELD else PACK - 1, PACK):
+                gather(PACK + t, picked1[c][:, t, :], starts[c], w)
+            if c < len(HELD):
+                bf = interleave(picked1[c][:], w, keep, held_tags[HELD[c]], 1)
+            else:
+                bf = interleave(picked1[c][:], w, work, "w_bf", 4)
+            quantize(bf, x_c[1][:, cols], x_s[1][:, cols])
+
+        def products(c):
+            w = CHUNKS[c]
+            cols = slice(starts[c], starts[c] + w)
+            res = work.tile([P, PACK, w], F32, name="res", tag="w1_raw", bufs=3)
+            per = PER_BANK[c]
+            first = 4 + sum(2 * PACK // n for n in PER_BANK[:c])
+            for part in range(PACK // per):
+                pre = bank((first + 2 * part) % 8)
+                base = bank((first + 2 * part + 1) % 8)
+                for b in range(2):
+                    for e in range(per):
+                        ns = slice((per * part + e) * P, (per * part + e + 1) * P)
+                        nc.tensor.matmul_mx(
+                            out=pre[:, e * w : (e + 1) * w],
+                            lhsT=w2_c[:, b, ns].bitcast(FP8X4), lhsT_scale=w2_s[:, b, ns],
+                            rhs=x_c[b][:, cols].bitcast(FP8X4), rhs_scale=x_s[b][:, cols],
+                            start=(b == 0 and e == 0), stop=(b == 1 and e == per - 1),
+                        )
+                for b in range(2):
+                    for e in range(per):
+                        g = per * part + e
+                        nc.tensor.matmul_mx(
+                            out=base[:, e * w : (e + 1) * w],
+                            lhsT=w4_c[:, b, 2 * g * P : 2 * (g + 1) * P].bitcast(FP4X4),
+                            lhsT_scale=w4_s[:, b, g * P : (g + 1) * P],
+                            rhs=x_c[b][:, cols].bitcast(FP8X4), rhs_scale=x_s[b][:, cols],
+                            start=(b == 0 and e == 0), stop=(b == 1 and e == per - 1),
+                        )
+                for e in range(per):
+                    g = per * part + e
+                    nc.scalar.activation(res[:, g, :], pre[:, e * w : (e + 1) * w], ACT.Tanh, bias=bias[:, g : g + 1])
+                both = res[:, per * part : per * (part + 1), :].rearrange("p g m -> p (g m)")
+                nc.vector.tensor_tensor(both, base[:, : per * w], both, ADD)
+            nc.sync.dma_start(out_rows[:, :, cols], res[:])
+
+        for c in range(len(CHUNKS) + LAG):
+            if c < len(CHUNKS):
+                finish_x(c)
+            if c >= LAG:
+                products(c - LAG)

@@ -22,18 +22,43 @@ ADD = mybir.AluOpType.add
 P = 128
 PACK = 4
 K_PASS = P * PACK
+PASSES = 2
 BANK = 512
+BANKS = 8
+LIST_ROWS = 16
+QUADRANT = 32
+QUADRANTS = (0, 2, 1, 3)
 SLICES = H // P
+UNITS = S // BANK
+PIECE = 256
+
 TWO_PI = 2.0 * math.pi
 MAGIC = 98304.0
 MAGIC_BITS = float(0x47C00000)
 BITS_PER_TURN = 128.0
+
+PRODUCT_BANKS = 4
+SUM_BANKS = 2
+UNIT_BUFS = 2
+PAGE_BUFS = 5
+W1_BUFS = 3
+BF_BUFS = 4
+
 CHUNKS = (128, 256, 256, 256, 128)
-HELD = (3, 4)
-FIRST_UNITS = (256, 256, 512)
-UNITS = (512, 512)
-LAG = 1
+LATE = (3, 4)
+EARLY_COLUMNS = sum(CHUNKS[: LATE[0]])
 PER_BANK = (4, 2, 2, 2, 2)
+
+KIB = 1024
+AT_TABLE = (0, 16 * KIB)
+AT_FIRST_BF = AT_TABLE[1] + 3 * KIB // 2
+AT_SECOND_CODES = (AT_TABLE[1] + KIB, AT_TABLE[1] + 2 * KIB)
+AT_GAINED = AT_TABLE[1] + 3 * KIB
+AT_SECOND_BF = (AT_TABLE[1] + 8 * KIB, AT_TABLE[1] + 10 * KIB)
+AT_WGS = tuple((32 + 4 * t) * KIB for t in range(PACK))
+AT_X0_CODES = AT_WGS[3] - 2 * KIB
+AT_W2_CODES = AT_WGS[3] + 2 * KIB
+AT_LATE = dict(zip(LATE, AT_WGS))
 
 
 def tile_list_floor_suction_reading_kernel(
@@ -49,65 +74,67 @@ def tile_list_floor_suction_reading_kernel(
         def bank(i):
             return psum.tile([P, BANK], F32, name="bank%d" % i)
 
-        idx1 = keep.tile([P, S // 16], U16, name="idx1")
-        idx2 = keep.tile([P, S // 16], U16, name="idx2")
-        idx3 = keep.tile([P, M // 16], U16, name="idx3")
+        idx1 = keep.tile([P, S // LIST_ROWS], U16, name="idx1")
+        idx2 = keep.tile([P, S // LIST_ROWS], U16, name="idx2")
+        idx3 = keep.tile([P, M // LIST_ROWS], U16, name="idx3")
 
         tab_s = keep.tile([P, T], U8, name="tab_s", tag="v_w1", align_bytes=64)
         nc.vector.memset(tab_s[:].bitcast(I32), 0)
         nc.sync.dma_start(idx1[:], offs)
+        for q in QUADRANTS:
+            live = slice(QUADRANT * q, QUADRANT * q + PASSES * PACK)
+            nc.gpsimd.dma_start(tab_s[live, :].bitcast(I32), tab_scales[:, 4 * q : 4 * q + 4, :].bitcast(I32))
         tab_w = []
-        for a in range(2):
-            t_ = shared.tile([P, T], I32, name="tab_w%d" % a, align_bytes=64, offset=4 * T * a)
-            nc.sync.dma_start(t_[:], tab_words[a].rearrange("p t i -> p (t i)").bitcast(I32))
-            tab_w.append(t_)
-        for q in range(4):
-            nc.gpsimd.dma_start(
-                tab_s[32 * q : 32 * q + 8, :].bitcast(I32), tab_scales[:, 4 * q : 4 * q + 4, :].bitcast(I32)
-            )
-
-        def load_w1(a, b):
-            raw = work.tile([P, PACK, K_PASS], F32, name="w1_raw", tag="w1_raw", bufs=3)
-            rows = w1[a * K_PASS : (a + 1) * K_PASS, b * K_PASS : (b + 1) * K_PASS]
-            nc.sync.dma_start(raw[:], rows.rearrange("(p i) c -> p i c", i=PACK))
-            return raw
-
-        page_rows = page0.rearrange("(b p t) c -> b t p c", b=2, t=PACK)
-
-        def load_page(s):
-            pg = work.tile([P, T2], F32, name="page", bufs=5)
-            nc.sync.dma_start(pg[:], page_rows[s // PACK, s % PACK])
-            return pg
+        for a in range(PASSES):
+            words = shared.tile([P, T], I32, name="tab_w%d" % a, align_bytes=64, offset=AT_TABLE[a])
+            nc.sync.dma_start(words[:], tab_words[a].rearrange("p t i -> p (t i)").bitcast(I32))
+            tab_w.append(words)
 
         w1_raw = {}
         pages = {}
-        w1_raw[0, 0] = load_w1(0, 0)
-        w1_raw[1, 0] = load_w1(1, 0)
-        gains = keep.tile([P, 2, PACK], F32, name="gains")
-        nc.sync.dma_start(gains[:], gain.rearrange("(b p t) -> p b t", b=2, t=PACK))
+        page_rows = page0.rearrange("(b p t) c -> b t p c", b=PASSES, t=PACK)
         wgs_rows = wgs.rearrange("(p t) j -> p t j", t=PACK)
-        wgs_first = keep.tile([P, S], F32, name="wgs_first", tag="wgs_first", align_bytes=64)
-        wgs_rest = keep.tile([P, PACK - 1, S], F32, name="wgs_rest", tag="wgs_rest", align_bytes=64)
-        for q in (0, 2, 1, 3):
-            nc.sync.dma_start(wgs_first[32 * q : 32 * q + 32, :], wgs_rows[:, 0, :])
+
+        def load_w1(a, b):
+            raw = work.tile([P, PACK, K_PASS], F32, name="w1_raw", tag="w1_raw", bufs=W1_BUFS)
+            rows = w1[a * K_PASS : (a + 1) * K_PASS, b * K_PASS : (b + 1) * K_PASS]
+            nc.sync.dma_start(raw[:], rows.rearrange("(p i) c -> p i c", i=PACK))
+            w1_raw[a, b] = raw
+
+        def load_page(s):
+            page = work.tile([P, T2], F32, name="page", bufs=PAGE_BUFS)
+            nc.sync.dma_start(page[:], page_rows[s // PACK, s % PACK])
+            pages[s] = page
+
+        def load_wgs(t):
+            for q in QUADRANTS:
+                nc.sync.dma_start(wgs_sb[t][QUADRANT * q : QUADRANT * (q + 1), :], wgs_rows[:, t, :])
+
+        load_w1(0, 0)
+        load_w1(1, 0)
+        gains = keep.tile([P, PASSES, PACK], F32, name="gains")
+        nc.sync.dma_start(gains[:], gain.rearrange("(b p t) -> p b t", b=PASSES, t=PACK))
+        wgs_sb = [shared.tile([P, S], F32, name="wgs%d" % t, align_bytes=64, offset=AT_WGS[t]) for t in range(PACK)]
+        load_wgs(0)
         nc.sync.dma_start(idx2[:], offs2)
-        pages[0] = load_page(0)
+        load_page(0)
+        load_wgs(1)
+        load_page(1)
         wgt_sb = keep.tile([P, M], F32, name="wgt_sb")
         nc.sync.dma_start(wgt_sb[:], wgt)
         nc.sync.dma_start(idx3[:], offs3)
-        for q in (0, 2, 1, 3):
-            nc.sync.dma_start(wgs_rest[32 * q : 32 * q + 32, :, :], wgs_rows[:, 1:, :])
-        pages[1] = load_page(1)
-        pages[2] = load_page(2)
-        w1_raw[0, 1] = load_w1(0, 1)
-        w1_raw[1, 1] = load_w1(1, 1)
+        load_wgs(2)
+        load_page(2)
+        load_w1(0, 1)
+        load_w1(1, 1)
+        load_wgs(3)
 
         ident = keep.tile([P, P], F32, name="ident")
         make_identity(nc, ident[:])
         neg_magic = keep.tile([P, P], F32, name="neg_magic")
         nc.gpsimd.memset(neg_magic[:], -MAGIC)
 
-        v_w = [keep.tile([P, S], U32, name="v_w", tag="v_w%d" % a, align_bytes=64) for a in range(2)]
+        v_w = [keep.tile([P, S], U32, name="v_w", tag="v_w%d" % a, align_bytes=64) for a in range(PASSES)]
         v_s = keep.tile([P, S], U8, name="v_s", align_bytes=64)
         nc.vector.tensor_copy(v_w[0][:], tab_w[0][:].bitcast(U32).indirect(idx1[:]))
         nc.vector.tensor_copy(v_s[:], tab_s[:].indirect(idx1[:]))
@@ -117,237 +144,248 @@ def tile_list_floor_suction_reading_kernel(
         w1_s = {}
         w1_bf = {}
 
-        first_bf = shared.tile([P, 4, 2, P, PACK], BF16, name="first_bf", align_bytes=64, offset=4 * T)
-
         def cast_w1(a, b, u):
             if b == 0:
-                bf = first_bf[:, 2 * a + u]
+                at = AT_FIRST_BF if u == 0 else AT_SECOND_BF[a]
+                bf = shared.tile([P, 2, P, PACK], BF16, name="first_bf%d%d" % (a, u), align_bytes=64, offset=at)
             else:
-                bf = work.tile([P, 2, P, PACK], BF16, name="w_bf", tag="w_bf", bufs=4, align_bytes=64)[:]
+                bf = work.tile([P, 2, P, PACK], BF16, name="w_bf", tag="w_bf", bufs=BF_BUFS, align_bytes=64)
             src = w1_raw[a, b][:].rearrange("p i (q t) -> p q i t", t=PACK)[:, :, :, 2 * u : 2 * u + 2]
-            dst = bf.rearrange("p t q i -> p q i t")
-            if b == 0:
+            dst = bf[:].rearrange("p e q i -> p q i e")
+            if (b, u) == (0, 0):
                 nc.vector.tensor_copy(dst, src)
             else:
                 nc.scalar.copy(dst, src)
             w1_bf[a, b, u] = bf
 
-        def quant_w1(a, b, u):
-            c_ = keep.tile([P, 2 * P], U32, name="w1_c", tag="w1_c%d%d%d" % (a, b, u), align_bytes=64)
-            s_ = keep.tile([P, 2 * P], U8, name="w1_s", tag="w1_s%d%d%d" % (a, b, u), align_bytes=64)
+        def quantize_w1(a, b, u):
+            if (b, u) == (0, 1):
+                codes = shared.tile([P, 2 * P], U32, name="w1_c%d" % a, align_bytes=64, offset=AT_SECOND_CODES[a])
+            else:
+                codes = keep.tile([P, 2 * P], U32, name="w1_c", tag="w1_c%d%d%d" % (a, b, u), align_bytes=64)
+            scales = keep.tile([P, 2 * P], U8, name="w1_s", tag="w1_s%d%d%d" % (a, b, u), align_bytes=64)
             nc.vector.quantize_mx(
-                out=c_[:].bitcast(FP8X4), scales=s_[:], in_=w1_bf[a, b, u].rearrange("p t q i -> p (t q i)")
+                out=codes[:].bitcast(FP8X4), scales=scales[:], in_=w1_bf[a, b, u][:].rearrange("p e q i -> p (e q i)")
             )
-            w1_c[a, b, u] = c_
-            w1_s[a, b, u] = s_
+            w1_c[a, b, u] = codes
+            w1_s[a, b, u] = scales
 
         for u in range(2):
-            for a in range(2):
+            for a in range(PASSES):
                 cast_w1(a, 0, u)
-                quant_w1(a, 0, u)
-        gained = shared.tile([P, S], F32, name="gained", align_bytes=64, offset=6 * T)
-        nc.vector.tensor_scalar(gained[:], wgs_first[:], gains[:, 0, 0:1], None, MULT)
+                quantize_w1(a, 0, u)
+        gained = shared.tile([P, S], F32, name="gained", align_bytes=64, offset=AT_GAINED)
+        for half in range(UNITS):
+            js = slice(half * BANK, (half + 1) * BANK)
+            nc.vector.tensor_scalar(gained[:, js], wgs_sb[0][:, js], gains[:, 0, 0:1], None, MULT)
 
-        def sine_unit(s, n, j0, width, sin_t):
+        def split_angle(unit, z):
+            whole = keep.tile([P, BANK], U32, name="whole", tag="whole%d" % (unit % UNIT_BUFS), align_bytes=64)
+            turns = keep.tile([P, BANK], F32, name="turns", tag="turns%d" % (unit % UNIT_BUFS), align_bytes=64)
+            nc.scalar.activation(whole[:], z[:], ACT.Copy, bias=MAGIC_BITS, scale=-BITS_PER_TURN / TWO_PI)
+            nc.scalar.activation(turns[:], z[:], ACT.Copy, scale=1.0 / TWO_PI)
+            return whole, turns
+
+        def first_slice_unit(half, sines):
+            js = slice(half * BANK, (half + 1) * BANK)
+            z = bank(half % PRODUCT_BANKS)
+            for a in range(PASSES):
+                nc.tensor.matmul_mx(
+                    out=z[:],
+                    lhsT=w1_c[a, 0, 0][:, :P].bitcast(FP8X4),
+                    lhsT_scale=w1_s[a, 0, 0][:, :P],
+                    rhs=v_w[a][:, js].bitcast(FP8X4),
+                    rhs_scale=v_s[PACK * a :, js],
+                    start=(a == 0),
+                    stop=(a == PASSES - 1),
+                )
+            whole, turns = split_angle(half, z)
+            nc.vector.scalar_tensor_tensor(turns[:], whole[:].bitcast(F32), -MAGIC, turns[:], ADD, ADD)
+            nc.scalar.activation(sines[:, js], turns[:], ACT.Sin, scale=TWO_PI)
+
+        def later_slice_unit(s, half, sines):
             b, t = divmod(s, PACK)
             u, e = divmod(t, 2)
-            cols = slice(e * P, (e + 1) * P)
-            tiles = width // P
-            z = bank(n % 2)
-            for a in range(2):
-                for jt in range(tiles):
-                    js = slice(j0 + jt * P, j0 + (jt + 1) * P)
+            unit = UNITS * s + half
+            rows = slice(e * P, (e + 1) * P)
+            blocks = BANK // P
+            z = bank(unit % PRODUCT_BANKS)
+            for a in range(PASSES):
+                for block in range(blocks):
+                    js = slice(half * BANK + block * P, half * BANK + (block + 1) * P)
                     nc.tensor.matmul_mx(
-                        out=z[:, jt * P : (jt + 1) * P],
+                        out=z[:, block * P : (block + 1) * P],
                         lhsT=v_w[a][:, js].bitcast(FP8X4),
-                        lhsT_scale=v_s[4 * a :, js],
-                        rhs=w1_c[a, b, u][:, cols].bitcast(FP8X4),
-                        rhs_scale=w1_s[a, b, u][:, cols],
-                        start=(a == 0 and jt == 0),
-                        stop=(a == 1 and jt == tiles - 1),
+                        lhsT_scale=v_s[PACK * a :, js],
+                        rhs=w1_c[a, b, u][:, rows].bitcast(FP8X4),
+                        rhs_scale=w1_s[a, b, u][:, rows],
+                        start=(a == 0 and block == 0),
+                        stop=(a == PASSES - 1 and block == blocks - 1),
                     )
-            whole = work.tile([P, BANK], U32, name="whole")
-            turns = work.tile([P, BANK], F32, name="turns")
-            nc.scalar.activation(
-                whole[:, :width], z[:, :width], ACT.Copy, bias=MAGIC_BITS, scale=-BITS_PER_TURN / TWO_PI
-            )
-            nc.scalar.activation(turns[:, :width], z[:, :width], ACT.Copy, scale=1.0 / TWO_PI)
-            r = bank(2 + n % 2)
-            for term in range(3):
-                for jt in range(tiles):
-                    js = slice(jt * P, (jt + 1) * P)
-                    src = (neg_magic[:], whole[:, js].bitcast(F32), turns[:, js])[term]
+            whole, turns = split_angle(unit, z)
+            reduced = bank(PRODUCT_BANKS + unit % SUM_BANKS)
+            terms = 3
+            for term in range(terms):
+                for block in range(blocks):
+                    cols = slice(block * P, (block + 1) * P)
                     nc.tensor.matmul(
-                        r[:, js], src, ident[:], is_transpose=True,
-                        start=(term == 0 and jt == 0), stop=(term == 2 and jt == tiles - 1),
+                        reduced[:, cols],
+                        (neg_magic[:], whole[:, cols].bitcast(F32), turns[:, cols])[term],
+                        ident[:],
+                        is_transpose=True,
+                        start=(term == 0 and block == 0),
+                        stop=(term == terms - 1 and block == blocks - 1),
                     )
-            part = sin_t[:, j0 : j0 + width]
-            nc.scalar.activation(part, r[:, :width], ACT.Sin, scale=TWO_PI)
-            if s > 0:
-                nc.scalar.activation(part, part, ACT.Copy, scale=gains[:, b, t : t + 1])
+            part = sines[:, half * BANK : (half + 1) * BANK]
+            nc.scalar.activation(part, reduced[:], ACT.Sin, scale=TWO_PI)
+            nc.scalar.activation(part, part, ACT.Copy, scale=gains[:, b, t : t + 1])
 
+        picked = [keep.tile([P, PACK, M], F32, name="picked%d" % b, align_bytes=64) for b in range(PASSES)]
         starts = [sum(CHUNKS[:c]) for c in range(len(CHUNKS))]
-        picked0 = []
-        picked1 = {
-            c: keep.tile([P, PACK, w], F32, name="picked1_%d" % c) for c, w in enumerate(CHUNKS) if c not in HELD
-        }
 
-        def gather(s, dst, m0, w):
-            lists = idx3[:, m0 // 16 : (m0 + w) // 16]
-            nc.vector.tensor_tensor(dst, pages[s][:].indirect(lists), wgt_sb[:, m0 : m0 + w], MULT)
+        def gather(s, dst, m0, width):
+            lists = idx3[:, m0 // LIST_ROWS : (m0 + width) // LIST_ROWS]
+            nc.vector.tensor_tensor(dst, pages[s][:].indirect(lists), wgt_sb[:, m0 : m0 + width], MULT)
 
         def gather_early(s):
             b, t = divmod(s, PACK)
-            if b == 0:
-                if t == 0:
-                    picked0.append(shared.tile([P, PACK, M], F32, name="picked0", align_bytes=64, offset=4 * T))
-                gather(s, picked0[0][:, t, :], 0, M)
-            else:
-                for c, w in enumerate(CHUNKS):
-                    if c not in HELD:
-                        gather(s, picked1[c][:, t, :], starts[c], w)
+            width = M if b == 0 else EARLY_COLUMNS
+            gather(s, picked[b][:, t, :width], 0, width)
 
-        def interleave(src, w, pool, tag, bufs):
-            bf = pool.tile([P, w, PACK], BF16, name="x_bf", tag=tag, bufs=bufs, align_bytes=64)
-            nc.scalar.copy(
-                bf[:].rearrange("p (c i) t -> p c t i", i=4), src.rearrange("p t (c i) -> p c t i", i=4)
-            )
+        def interleave(src, width, pool, tag, bufs, offset=None):
+            bf = pool.tile([P, width, PACK], BF16, name="x_bf", tag=tag, bufs=bufs, align_bytes=64, offset=offset)
+            nc.scalar.copy(bf[:].rearrange("p (c i) t -> p c t i", i=4), src.rearrange("p t (c i) -> p c t i", i=4))
             return bf
 
         def quantize(bf, codes, scales):
             nc.vector.quantize_mx(out=codes.bitcast(FP8X4), scales=scales, in_=bf[:].rearrange("p c t -> p (c t)"))
 
-        x_c = {1: keep.tile([P, M], U32, name="x_c1", align_bytes=64)}
-        x_s = [keep.tile([P, M], U8, name="x_s%d" % b, align_bytes=64) for b in range(2)]
+        x1_c = keep.tile([P, M], U32, name="x1_c", align_bytes=64)
+        x_s = [keep.tile([P, M], U8, name="x_s%d" % b, align_bytes=64) for b in range(PASSES)]
+        w2_s = keep.tile([P, PASSES, N], U8, name="w2_s", align_bytes=64)
+        w4_c = keep.tile([P, PASSES, 2 * N], U8, name="w4_c", align_bytes=64)
+        w4_s = keep.tile([P, PASSES, N], U8, name="w4_s", align_bytes=64)
+        bias = keep.tile([P, N // P], F32, name="bias")
+
+        load_page(3)
+        load_page(4)
+        w2_raw = shared.tile([P, PASSES, PACK, N], F32, name="w2_raw", align_bytes=64, offset=AT_TABLE[0])
+        for b in range(PASSES):
+            rows = w2[b * K_PASS : (b + 1) * K_PASS, :]
+            nc.sync.dma_start(w2_raw[:, b], rows.rearrange("(p i) n -> p i n", i=PACK))
+        nc.sync.dma_start(w4_c[:].bitcast(I32), w4_words.rearrange("b p n -> p b n").bitcast(I32))
+        nc.gpsimd.memset(w4_s[:].bitcast(I32), 0)
+        for q in range(P // QUADRANT):
+            nc.sync.dma_start(
+                w4_s[QUADRANT * q : QUADRANT * q + 4].bitcast(I32),
+                w4_scales[:, 4 * q : 4 * q + 4, :].rearrange("b r n -> r b n").bitcast(I32),
+            )
+        with nc.allow_non_contiguous_dma(reason="one bias value a partition"):
+            nc.sync.dma_start(bias[:], b2.rearrange("(g p) -> p g", p=P))
+
+        first_sines = keep.tile([P, S], F32, name="first_sines", align_bytes=64)
+        for half in range(UNITS):
+            first_slice_unit(half, first_sines)
+        for half in range(UNITS):
+            js = slice(half * BANK, (half + 1) * BANK)
+            lists = idx2[:, half * BANK // LIST_ROWS : (half + 1) * BANK // LIST_ROWS]
+            nc.vector.tensor_tensor(pages[0][:].indirect(lists), first_sines[:, js], gained[:, js], MULT)
+        for s in range(1, SLICES):
+            sines = picked[(s - 1) // PACK][:, (s - 1) % PACK, :]
+            for half in range(UNITS):
+                later_slice_unit(s, half, sines)
+            nc.vector.tensor_tensor(pages[s][:].indirect(idx2[:]), sines, wgs_sb[s % PACK][:], MULT)
+            gather_early(s - 1)
+            if s - 1 + PAGE_BUFS < SLICES:
+                load_page(s - 1 + PAGE_BUFS)
+            if s <= 2:
+                for a in range(PASSES):
+                    cast_w1(a, 1, s - 1)
+                for a in range(PASSES):
+                    quantize_w1(a, 1, s - 1)
+
+        pieces = N // PIECE
         w2_bf = []
-        w2_s = keep.tile([P, 2, N], U8, name="w2_s", align_bytes=64)
-        w4_c = keep.tile([P, 2, 2 * N], U8, name="w4_c", align_bytes=64)
-        w4_s = keep.tile([P, 2, N], U8, name="w4_s", align_bytes=64)
-        bias = keep.tile([P, PACK], F32, name="bias")
-        w2_raw = []
+        for b in range(PASSES):
+            for h in range(pieces):
+                tag = ("whole%d", "turns%d")[b] % h
+                w2_bf.append(interleave(w2_raw[:, b, :, h * PIECE : (h + 1) * PIECE], PIECE, keep, tag, 1))
+        w2_c = shared.tile([P, PASSES, N], U32, name="w2_c", align_bytes=64, offset=AT_W2_CODES)
+        for n, bf in enumerate(w2_bf):
+            b, h = divmod(n, pieces)
+            cols = slice(h * PIECE, (h + 1) * PIECE)
+            quantize(bf, w2_c[:, b, cols], w2_s[:, b, cols])
+        x_c = [shared.tile([P, M], U32, name="x0_c", align_bytes=64, offset=AT_X0_CODES), x1_c]
+        out_rows = out.rearrange("(g p) m -> p g m", p=P)
 
-        def load_second():
-            raw = shared.tile([P, 2, PACK, N], F32, name="w2_raw", align_bytes=64, offset=0)
-            for b in range(2):
-                nc.sync.dma_start(
-                    raw[:, b], w2[b * K_PASS : (b + 1) * K_PASS, :].rearrange("(p i) n -> p i n", i=PACK)
-                )
-            w2_raw.append(raw)
-            nc.sync.dma_start(w4_c[:].bitcast(I32), w4_words.rearrange("b p n -> p b n").bitcast(I32))
-            nc.gpsimd.memset(w4_s[:].bitcast(I32), 0)
-            for q in range(4):
-                nc.sync.dma_start(
-                    w4_s[32 * q : 32 * q + 4].bitcast(I32),
-                    w4_scales[:, 4 * q : 4 * q + 4, :].rearrange("b r n -> r b n").bitcast(I32),
-                )
-            with nc.allow_non_contiguous_dma(reason="one bias value a partition"):
-                nc.sync.dma_start(bias[:], b2.rearrange("(g p) -> p g", p=P))
-
-        def quant_w2(b):
-            for h in range(2):
-                cols = slice(h * 256, (h + 1) * 256)
-                w2_bf.append(interleave(w2_raw[0][:, b, :, cols], 256, work, "w2_bf", 4))
-
-        def quant_x0(h):
-            for c in (2 * h, 2 * h + 1):
-                cols = slice(c * 256, (c + 1) * 256)
-                bf = interleave(picked0[0][:, :, cols], 256, keep, ("w1_c010", "w1_c110", "w1_s010", "w1_s110")[c], 1)
+        def quantize_x0():
+            for h, tag in enumerate(("w1_c011", "w1_c111", "w1_s011", "w1_s111")):
+                cols = slice(h * PIECE, (h + 1) * PIECE)
+                bf = interleave(picked[0][:, :, cols], PIECE, keep, tag, 1)
                 quantize(bf, x_c[0][:, cols], x_s[0][:, cols])
 
-        load_second()
-        pages[3] = load_page(3)
-        pages[4] = load_page(4)
-
-        unit = 0
-        for s in range(SLICES):
-            b, t = divmod(s, PACK)
-            sin_t = keep.tile([P, S], F32, name="sin_t", tag="sin%d" % (s % 3), align_bytes=64)
-            gw = gained[:] if s == 0 else wgs_first[:] if t == 0 else wgs_rest[:, t - 1, :]
-            widths = FIRST_UNITS if s == 0 else UNITS
-            for n, width in enumerate(widths):
-                sine_unit(s, unit, sum(widths[:n]), width, sin_t)
-                unit = unit + 1
-            if s == 0:
-                for n, width in enumerate(widths):
-                    j0 = sum(widths[:n])
-                    js = slice(j0, j0 + width)
-                    lists = idx2[:, j0 // 16 : (j0 + width) // 16]
-                    nc.vector.tensor_tensor(pages[s][:].indirect(lists), sin_t[:, js], gw[:, js], MULT)
+        def quantize_x1(c):
+            width = CHUNKS[c]
+            cols = slice(starts[c], starts[c] + width)
+            if c in LATE:
+                late = shared.tile([P, PACK, width], F32, name="late%d" % c, align_bytes=64, offset=AT_LATE[c])
+                for t in range(PACK):
+                    gather(PACK + t, late[:, t, :], starts[c], width)
+                src = late[:]
             else:
-                nc.vector.tensor_tensor(pages[s][:].indirect(idx2[:]), sin_t[:], gw, MULT)
-                gather_early(s - 1)
-            if 1 <= s <= 3:
-                pages[s + 4] = load_page(s + 4)
-            if s in (1, 2):
-                for a in range(2):
-                    cast_w1(a, 1, s - 1)
-                for a in range(2):
-                    quant_w1(a, 1, s - 1)
-            if s in (3, 4):
-                quant_w2(s - 3)
-            if s == 4:
-                w2_c = keep.tile([P, 2, N], U32, name="w2_c", tag="wgs_first", align_bytes=64)
-                for n, bf in enumerate(w2_bf):
-                    cols = slice(n % 2 * 256, (n % 2 + 1) * 256)
-                    quantize(bf, w2_c[:, n // 2, cols], w2_s[:, n // 2, cols])
-            if s == 5:
-                x_c[0] = keep.tile([P, M], U32, name="x_c0", tag="sin2", align_bytes=64)
-                quant_x0(0)
-                quant_x0(1)
-
-        out_rows = out.rearrange("(g p) m -> p g m", p=P)
-        held_tags = {HELD[0]: "sin1", HELD[1]: "wgs_rest"}
-
-        def finish_x(c):
-            w = CHUNKS[c]
-            cols = slice(starts[c], starts[c] + w)
-            if c in HELD:
-                picked1[c] = keep.tile([P, PACK, w], F32, name="picked1", tag=held_tags[c], align_bytes=64)
-            for t in range(0 if c in HELD else PACK - 1, PACK):
-                gather(PACK + t, picked1[c][:, t, :], starts[c], w)
-            if c < len(HELD):
-                bf = interleave(picked1[c][:], w, keep, held_tags[HELD[c]], 1)
+                src = picked[1][:, :, cols]
+            if c < len(LATE):
+                bf = interleave(src, width, shared, "x_bf%d" % c, 1, AT_LATE[LATE[c]])
             else:
-                bf = interleave(picked1[c][:], w, work, "w_bf", 4)
+                bf = interleave(src, width, work, "w_bf", BF_BUFS)
             quantize(bf, x_c[1][:, cols], x_s[1][:, cols])
 
         def products(c):
-            w = CHUNKS[c]
-            cols = slice(starts[c], starts[c] + w)
-            res = work.tile([P, PACK, w], F32, name="res", tag="w1_raw", bufs=3)
+            width = CHUNKS[c]
+            cols = slice(starts[c], starts[c] + width)
+            res = work.tile([P, N // P, width], F32, name="res", tag="w1_raw", bufs=W1_BUFS)
             per = PER_BANK[c]
-            first = 4 + sum(2 * PACK // n for n in PER_BANK[:c])
-            for part in range(PACK // per):
-                pre = bank((first + 2 * part) % 8)
-                base = bank((first + 2 * part + 1) % 8)
-                for b in range(2):
-                    for e in range(per):
-                        ns = slice((per * part + e) * P, (per * part + e + 1) * P)
-                        nc.tensor.matmul_mx(
-                            out=pre[:, e * w : (e + 1) * w],
-                            lhsT=w2_c[:, b, ns].bitcast(FP8X4), lhsT_scale=w2_s[:, b, ns],
-                            rhs=x_c[b][:, cols].bitcast(FP8X4), rhs_scale=x_s[b][:, cols],
-                            start=(b == 0 and e == 0), stop=(b == 1 and e == per - 1),
-                        )
-                for b in range(2):
+            first = PRODUCT_BANKS + sum(2 * (N // P) // n for n in PER_BANK[:c])
+            for part in range(N // P // per):
+                pre = bank((first + 2 * part) % BANKS)
+                base = bank((first + 2 * part + 1) % BANKS)
+                for b in range(PASSES):
                     for e in range(per):
                         g = per * part + e
                         nc.tensor.matmul_mx(
-                            out=base[:, e * w : (e + 1) * w],
+                            out=pre[:, e * width : (e + 1) * width],
+                            lhsT=w2_c[:, b, g * P : (g + 1) * P].bitcast(FP8X4),
+                            lhsT_scale=w2_s[:, b, g * P : (g + 1) * P],
+                            rhs=x_c[b][:, cols].bitcast(FP8X4),
+                            rhs_scale=x_s[b][:, cols],
+                            start=(b == 0 and e == 0),
+                            stop=(b == PASSES - 1 and e == per - 1),
+                        )
+                for b in range(PASSES):
+                    for e in range(per):
+                        g = per * part + e
+                        nc.tensor.matmul_mx(
+                            out=base[:, e * width : (e + 1) * width],
                             lhsT=w4_c[:, b, 2 * g * P : 2 * (g + 1) * P].bitcast(FP4X4),
                             lhsT_scale=w4_s[:, b, g * P : (g + 1) * P],
-                            rhs=x_c[b][:, cols].bitcast(FP8X4), rhs_scale=x_s[b][:, cols],
-                            start=(b == 0 and e == 0), stop=(b == 1 and e == per - 1),
+                            rhs=x_c[b][:, cols].bitcast(FP8X4),
+                            rhs_scale=x_s[b][:, cols],
+                            start=(b == 0 and e == 0),
+                            stop=(b == PASSES - 1 and e == per - 1),
                         )
                 for e in range(per):
                     g = per * part + e
-                    nc.scalar.activation(res[:, g, :], pre[:, e * w : (e + 1) * w], ACT.Tanh, bias=bias[:, g : g + 1])
-                both = res[:, per * part : per * (part + 1), :].rearrange("p g m -> p (g m)")
-                nc.vector.tensor_tensor(both, base[:, : per * w], both, ADD)
+                    nc.scalar.activation(
+                        res[:, g, :], pre[:, e * width : (e + 1) * width], ACT.Tanh, bias=bias[:, g : g + 1]
+                    )
+                bent = res[:, per * part : per * (part + 1), :].rearrange("p g m -> p (g m)")
+                nc.vector.tensor_tensor(bent, base[:, : per * width], bent, ADD)
             nc.sync.dma_start(out_rows[:, :, cols], res[:])
 
-        for c in range(len(CHUNKS) + LAG):
-            if c < len(CHUNKS):
-                finish_x(c)
-            if c >= LAG:
-                products(c - LAG)
+        gather_early(SLICES - 1)
+        quantize_x1(0)
+        quantize_x0()
+        for c in range(1, len(CHUNKS)):
+            quantize_x1(c)
+            products(c - 1)
+        products(len(CHUNKS) - 1)

@@ -134,6 +134,9 @@ def tile_list_floor_suction_reading_kernel(
         neg_magic = keep.tile([P, P], F32, name="neg_magic")
         nc.gpsimd.memset(neg_magic[:], -MAGIC)
 
+        warm = keep.tile([P, 8], F32, name="warm")
+        nc.scalar.activation(warm[:, 0:1], neg_magic[:, 0:1], ACT.Silu)
+
         v_w = [keep.tile([P, S], U32, name="v_w", tag="v_w%d" % a, align_bytes=64) for a in range(PASSES)]
         v_s = keep.tile([P, S], U8, name="v_s", align_bytes=64)
         nc.vector.tensor_copy(v_w[0][:], tab_w[0][:].bitcast(U32).indirect(idx1[:]))

import math
from contextlib import ExitStack

import concourse.mybir as mybir
from concourse.masks import make_identity

K, T, S, H, T2, M, N = 1024, 4096, 1024, 1024, 2048, 1024, 512
FLOPS = 2 * K * H * S + 2 * 2 * H * N * M

F32 = mybir.dt.float32
BF16 = mybir.dt.bfloat16
I32 = mybir.dt.int32
U32 = mybir.dt.uint32
U16 = mybir.dt.uint16
U8 = mybir.dt.uint8
FP8X4 = mybir.dt.float8_e4m3fn_x4
FP4X4 = mybir.dt.float4_e2m1fn_x4
ACT = mybir.ActivationFunctionType
MULT = mybir.AluOpType.mult
ADD = mybir.AluOpType.add

P = 128
PACK = 4
K_PASS = P * PACK
PASSES = 2
BANK = 512
BANKS = 8
LIST_ROWS = 16
QUADRANT = 32
QUADRANTS = (0, 2, 1, 3)
SLICES = H // P
UNITS = S // BANK
PIECE = 256

TWO_PI = 2.0 * math.pi
MAGIC = 98304.0
MAGIC_BITS = float(0x47C00000)
BITS_PER_TURN = 128.0

PRODUCT_BANKS = 4
SUM_BANKS = 2
UNIT_BUFS = 2
PAGE_BUFS = 5
W1_BUFS = 3
BF_BUFS = 4

CHUNKS = (128, 256, 256, 256, 128)
LATE = (3, 4)
EARLY_COLUMNS = sum(CHUNKS[: LATE[0]])
PER_BANK = (4, 2, 2, 2, 2)

KIB = 1024
AT_TABLE = (0, 16 * KIB)
AT_FIRST_BF = AT_TABLE[1] + 3 * KIB // 2
AT_SECOND_CODES = (AT_TABLE[1] + KIB, AT_TABLE[1] + 2 * KIB)
AT_GAINED = AT_TABLE[1] + 3 * KIB
AT_SECOND_BF = (AT_TABLE[1] + 8 * KIB, AT_TABLE[1] + 10 * KIB)
AT_WGS = tuple((32 + 4 * t) * KIB for t in range(PACK))
AT_X0_CODES = AT_WGS[3] - 2 * KIB
AT_W2_CODES = AT_WGS[3] + 2 * KIB
AT_LATE = dict(zip(LATE, AT_WGS))


def tile_list_floor_suction_reading_kernel(
    tc, tab_words, tab_scales, offs, w1, gain, page0, wgs, offs2, wgt, offs3, w4_words, w4_scales, w2, b2, out
):
    nc = tc.nc
    with ExitStack() as ctx:
        keep = ctx.enter_context(tc.tile_pool(name="keep", bufs=1))
        work = ctx.enter_context(tc.tile_pool(name="work", bufs=2))
        shared = ctx.enter_context(tc.tile_pool(name="shared", bufs=1))
        psum = ctx.enter_context(tc.psum_pool(name="psum", bufs=1))

        def bank(i):
            return psum.tile([P, BANK], F32, name="bank%d" % i)

        idx1 = keep.tile([P, S // LIST_ROWS], U16, name="idx1")
        idx2 = keep.tile([P, S // LIST_ROWS], U16, name="idx2")
        idx3 = keep.tile([P, M // LIST_ROWS], U16, name="idx3")

        tab_s = keep.tile([P, T], U8, name="tab_s", tag="v_w1", align_bytes=64)
        nc.vector.memset(tab_s[:].bitcast(I32), 0)
        nc.sync.dma_start(idx1[:], offs)
        for q in QUADRANTS:
            live = slice(QUADRANT * q, QUADRANT * q + PASSES * PACK)
            nc.gpsimd.dma_start(tab_s[live, :].bitcast(I32), tab_scales[:, 4 * q : 4 * q + 4, :].bitcast(I32))
        tab_w = []
        for a in range(PASSES):
            words = shared.tile([P, T], I32, name="tab_w%d" % a, align_bytes=64, offset=AT_TABLE[a])
            nc.sync.dma_start(words[:], tab_words[a].rearrange("p t i -> p (t i)").bitcast(I32))
            tab_w.append(words)

        w1_raw = {}
        pages = {}
        page_rows = page0.rearrange("(b p t) c -> b t p c", b=PASSES, t=PACK)
        wgs_rows = wgs.rearrange("(p t) j -> p t j", t=PACK)

        def load_w1(a, b):
            raw = work.tile([P, PACK, K_PASS], F32, name="w1_raw", tag="w1_raw", bufs=W1_BUFS)
            rows = w1[a * K_PASS : (a + 1) * K_PASS, b * K_PASS : (b + 1) * K_PASS]
            nc.sync.dma_start(raw[:], rows.rearrange("(p i) c -> p i c", i=PACK))
            w1_raw[a, b] = raw

        def load_page(s):
            page = work.tile([P, T2], F32, name="page", bufs=PAGE_BUFS)
            nc.sync.dma_start(page[:], page_rows[s // PACK, s % PACK])
            pages[s] = page

        def load_wgs(t):
            for q in QUADRANTS:
                nc.sync.dma_start(wgs_sb[t][QUADRANT * q : QUADRANT * (q + 1), :], wgs_rows[:, t, :])

        load_w1(0, 0)
        load_w1(1, 0)
        gains = keep.tile([P, PASSES, PACK], F32, name="gains")
        nc.sync.dma_start(gains[:], gain.rearrange("(b p t) -> p b t", b=PASSES, t=PACK))
        wgs_sb = [shared.tile([P, S], F32, name="wgs%d" % t, align_bytes=64, offset=AT_WGS[t]) for t in range(PACK)]
        load_wgs(0)
        nc.sync.dma_start(idx2[:], offs2)
        load_page(0)
        load_wgs(1)
        load_page(1)
        wgt_sb = keep.tile([P, M], F32, name="wgt_sb")
        nc.sync.dma_start(wgt_sb[:], wgt)
        nc.sync.dma_start(idx3[:], offs3)
        load_wgs(2)
        load_page(2)
        load_w1(0, 1)
        load_w1(1, 1)
        load_wgs(3)

        ident = keep.tile([P, P], F32, name="ident")
        make_identity(nc, ident[:])
        neg_magic = keep.tile([P, P], F32, name="neg_magic")
        nc.gpsimd.memset(neg_magic[:], -MAGIC)

        warm = keep.tile([P, 8], F32, name="warm")
        nc.scalar.activation(warm[:, 0:1], neg_magic[:, 0:1], ACT.Silu)

        v_w = [keep.tile([P, S], U32, name="v_w", tag="v_w%d" % a, align_bytes=64) for a in range(PASSES)]
        v_s = keep.tile([P, S], U8, name="v_s", align_bytes=64)
        nc.vector.tensor_copy(v_w[0][:], tab_w[0][:].bitcast(U32).indirect(idx1[:]))
        nc.vector.tensor_copy(v_s[:], tab_s[:].indirect(idx1[:]))
        nc.vector.tensor_copy(v_w[1][:], tab_w[1][:].bitcast(U32).indirect(idx1[:]))

        w1_c = {}
        w1_s = {}
        w1_bf = {}

        def cast_w1(a, b, u):
            if b == 0:
                at = AT_FIRST_BF if u == 0 else AT_SECOND_BF[a]
                bf = shared.tile([P, 2, P, PACK], BF16, name="first_bf%d%d" % (a, u), align_bytes=64, offset=at)
            else:
                bf = work.tile([P, 2, P, PACK], BF16, name="w_bf", tag="w_bf", bufs=BF_BUFS, align_bytes=64)
            src = w1_raw[a, b][:].rearrange("p i (q t) -> p q i t", t=PACK)[:, :, :, 2 * u : 2 * u + 2]
            dst = bf[:].rearrange("p e q i -> p q i e")
            if (b, u) == (0, 0):
                nc.vector.tensor_copy(dst, src)
            else:
                nc.scalar.copy(dst, src)
            w1_bf[a, b, u] = bf

        def quantize_w1(a, b, u):
            if (b, u) == (0, 1):
                codes = shared.tile([P, 2 * P], U32, name="w1_c%d" % a, align_bytes=64, offset=AT_SECOND_CODES[a])
            else:
                codes = keep.tile([P, 2 * P], U32, name="w1_c", tag="w1_c%d%d%d" % (a, b, u), align_bytes=64)
            scales = keep.tile([P, 2 * P], U8, name="w1_s", tag="w1_s%d%d%d" % (a, b, u), align_bytes=64)
            nc.vector.quantize_mx(
                out=codes[:].bitcast(FP8X4), scales=scales[:], in_=w1_bf[a, b, u][:].rearrange("p e q i -> p (e q i)")
            )
            w1_c[a, b, u] = codes
            w1_s[a, b, u] = scales

        for u in range(2):
            for a in range(PASSES):
                cast_w1(a, 0, u)
                quantize_w1(a, 0, u)
        gained = shared.tile([P, S], F32, name="gained", align_bytes=64, offset=AT_GAINED)
        for half in range(UNITS):
            js = slice(half * BANK, (half + 1) * BANK)
            nc.vector.tensor_scalar(gained[:, js], wgs_sb[0][:, js], gains[:, 0, 0:1], None, MULT)

        def split_angle(unit, z):
            whole = keep.tile([P, BANK], U32, name="whole", tag="whole%d" % (unit % UNIT_BUFS), align_bytes=64)
            turns = keep.tile([P, BANK], F32, name="turns", tag="turns%d" % (unit % UNIT_BUFS), align_bytes=64)
            nc.scalar.activation(whole[:], z[:], ACT.Copy, bias=MAGIC_BITS, scale=-BITS_PER_TURN / TWO_PI)
            nc.scalar.activation(turns[:], z[:], ACT.Copy, scale=1.0 / TWO_PI)
            return whole, turns

        def first_slice_unit(half, sines):
            js = slice(half * BANK, (half + 1) * BANK)
            z = bank(half % PRODUCT_BANKS)
            for a in range(PASSES):
                nc.tensor.matmul_mx(
                    out=z[:],
                    lhsT=w1_c[a, 0, 0][:, :P].bitcast(FP8X4),
                    lhsT_scale=w1_s[a, 0, 0][:, :P],
                    rhs=v_w[a][:, js].bitcast(FP8X4),
                    rhs_scale=v_s[PACK * a :, js],
                    start=(a == 0),
                    stop=(a == PASSES - 1),
                )
            whole, turns = split_angle(half, z)
            nc.vector.scalar_tensor_tensor(turns[:], whole[:].bitcast(F32), -MAGIC, turns[:], ADD, ADD)
            nc.scalar.activation(sines[:, js], turns[:], ACT.Sin, scale=TWO_PI)

        def later_slice_unit(s, half, sines):
            b, t = divmod(s, PACK)
            u, e = divmod(t, 2)
            unit = UNITS * s + half
            rows = slice(e * P, (e + 1) * P)
            blocks = BANK // P
            z = bank(unit % PRODUCT_BANKS)
            for a in range(PASSES):
                for block in range(blocks):
                    js = slice(half * BANK + block * P, half * BANK + (block + 1) * P)
                    nc.tensor.matmul_mx(
                        out=z[:, block * P : (block + 1) * P],
                        lhsT=v_w[a][:, js].bitcast(FP8X4),
                        lhsT_scale=v_s[PACK * a :, js],
                        rhs=w1_c[a, b, u][:, rows].bitcast(FP8X4),
                        rhs_scale=w1_s[a, b, u][:, rows],
                        start=(a == 0 and block == 0),
                        stop=(a == PASSES - 1 and block == blocks - 1),
                    )
            whole, turns = split_angle(unit, z)
            reduced = bank(PRODUCT_BANKS + unit % SUM_BANKS)
            terms = 3
            for term in range(terms):
                for block in range(blocks):
                    cols = slice(block * P, (block + 1) * P)
                    nc.tensor.matmul(
                        reduced[:, cols],
                        (neg_magic[:], whole[:, cols].bitcast(F32), turns[:, cols])[term],
                        ident[:],
                        is_transpose=True,
                        start=(term == 0 and block == 0),
                        stop=(term == terms - 1 and block == blocks - 1),
                    )
            part = sines[:, half * BANK : (half + 1) * BANK]
            nc.scalar.activation(part, reduced[:], ACT.Sin, scale=TWO_PI)
            nc.scalar.activation(part, part, ACT.Copy, scale=gains[:, b, t : t + 1])

        picked = [keep.tile([P, PACK, M], F32, name="picked%d" % b, align_bytes=64) for b in range(PASSES)]
        starts = [sum(CHUNKS[:c]) for c in range(len(CHUNKS))]

        def gather(s, dst, m0, width):
            lists = idx3[:, m0 // LIST_ROWS : (m0 + width) // LIST_ROWS]
            nc.vector.tensor_tensor(dst, pages[s][:].indirect(lists), wgt_sb[:, m0 : m0 + width], MULT)

        def gather_early(s):
            b, t = divmod(s, PACK)
            width = M if b == 0 else EARLY_COLUMNS
            gather(s, picked[b][:, t, :width], 0, width)

        def interleave(src, width, pool, tag, bufs, offset=None):
            bf = pool.tile([P, width, PACK], BF16, name="x_bf", tag=tag, bufs=bufs, align_bytes=64, offset=offset)
            nc.scalar.copy(bf[:].rearrange("p (c i) t -> p c t i", i=4), src.rearrange("p t (c i) -> p c t i", i=4))
            return bf

        def quantize(bf, codes, scales):
            nc.vector.quantize_mx(out=codes.bitcast(FP8X4), scales=scales, in_=bf[:].rearrange("p c t -> p (c t)"))

        x1_c = keep.tile([P, M], U32, name="x1_c", align_bytes=64)
        x_s = [keep.tile([P, M], U8, name="x_s%d" % b, align_bytes=64) for b in range(PASSES)]
        w2_s = keep.tile([P, PASSES, N], U8, name="w2_s", align_bytes=64)
        w4_c = keep.tile([P, PASSES, 2 * N], U8, name="w4_c", align_bytes=64)
        w4_s = keep.tile([P, PASSES, N], U8, name="w4_s", align_bytes=64)
        bias = keep.tile([P, N // P], F32, name="bias")

        load_page(3)
        load_page(4)
        w2_raw = shared.tile([P, PASSES, PACK, N], F32, name="w2_raw", align_bytes=64, offset=AT_TABLE[0])
        for b in range(PASSES):
            rows = w2[b * K_PASS : (b + 1) * K_PASS, :]
            nc.sync.dma_start(w2_raw[:, b], rows.rearrange("(p i) n -> p i n", i=PACK))
        nc.sync.dma_start(w4_c[:].bitcast(I32), w4_words.rearrange("b p n -> p b n").bitcast(I32))
        nc.gpsimd.memset(w4_s[:].bitcast(I32), 0)
        for q in range(P // QUADRANT):
            nc.sync.dma_start(
                w4_s[QUADRANT * q : QUADRANT * q + 4].bitcast(I32),
                w4_scales[:, 4 * q : 4 * q + 4, :].rearrange("b r n -> r b n").bitcast(I32),
            )
        with nc.allow_non_contiguous_dma(reason="one bias value a partition"):
            nc.sync.dma_start(bias[:], b2.rearrange("(g p) -> p g", p=P))

        first_sines = keep.tile([P, S], F32, name="first_sines", align_bytes=64)
        for half in range(UNITS):
            first_slice_unit(half, first_sines)
        for half in range(UNITS):
            js = slice(half * BANK, (half + 1) * BANK)
            lists = idx2[:, half * BANK // LIST_ROWS : (half + 1) * BANK // LIST_ROWS]
            nc.vector.tensor_tensor(pages[0][:].indirect(lists), first_sines[:, js], gained[:, js], MULT)
        for s in range(1, SLICES):
            sines = picked[(s - 1) // PACK][:, (s - 1) % PACK, :]
            for half in range(UNITS):
                later_slice_unit(s, half, sines)
            nc.vector.tensor_tensor(pages[s][:].indirect(idx2[:]), sines, wgs_sb[s % PACK][:], MULT)
            gather_early(s - 1)
            if s - 1 + PAGE_BUFS < SLICES:
                load_page(s - 1 + PAGE_BUFS)
            if s <= 2:
                for a in range(PASSES):
                    cast_w1(a, 1, s - 1)
                for a in range(PASSES):
                    quantize_w1(a, 1, s - 1)

        pieces = N // PIECE
        w2_bf = []
        for b in range(PASSES):
            for h in range(pieces):
                tag = ("whole%d", "turns%d")[b] % h
                w2_bf.append(interleave(w2_raw[:, b, :, h * PIECE : (h + 1) * PIECE], PIECE, keep, tag, 1))
        w2_c = shared.tile([P, PASSES, N], U32, name="w2_c", align_bytes=64, offset=AT_W2_CODES)
        for n, bf in enumerate(w2_bf):
            b, h = divmod(n, pieces)
            cols = slice(h * PIECE, (h + 1) * PIECE)
            quantize(bf, w2_c[:, b, cols], w2_s[:, b, cols])
        x_c = [shared.tile([P, M], U32, name="x0_c", align_bytes=64, offset=AT_X0_CODES), x1_c]
        out_rows = out.rearrange("(g p) m -> p g m", p=P)

        def quantize_x0():
            for h, tag in enumerate(("w1_c011", "w1_c111", "w1_s011", "w1_s111")):
                cols = slice(h * PIECE, (h + 1) * PIECE)
                bf = interleave(picked[0][:, :, cols], PIECE, keep, tag, 1)
                quantize(bf, x_c[0][:, cols], x_s[0][:, cols])

        def quantize_x1(c):
            width = CHUNKS[c]
            cols = slice(starts[c], starts[c] + width)
            if c in LATE:
                late = shared.tile([P, PACK, width], F32, name="late%d" % c, align_bytes=64, offset=AT_LATE[c])
                for t in range(PACK):
                    gather(PACK + t, late[:, t, :], starts[c], width)
                src = late[:]
            else:
                src = picked[1][:, :, cols]
            if c < len(LATE):
                bf = interleave(src, width, shared, "x_bf%d" % c, 1, AT_LATE[LATE[c]])
            else:
                bf = interleave(src, width, work, "w_bf", BF_BUFS)
            quantize(bf, x_c[1][:, cols], x_s[1][:, cols])

        def products(c):
            width = CHUNKS[c]
            cols = slice(starts[c], starts[c] + width)
            res = work.tile([P, N // P, width], F32, name="res", tag="w1_raw", bufs=W1_BUFS)
            per = PER_BANK[c]
            first = PRODUCT_BANKS + sum(2 * (N // P) // n for n in PER_BANK[:c])
            for part in range(N // P // per):
                pre = bank((first + 2 * part) % BANKS)
                base = bank((first + 2 * part + 1) % BANKS)
                for b in range(PASSES):
                    for e in range(per):
                        g = per * part + e
                        nc.tensor.matmul_mx(
                            out=pre[:, e * width : (e + 1) * width],
                            lhsT=w2_c[:, b, g * P : (g + 1) * P].bitcast(FP8X4),
                            lhsT_scale=w2_s[:, b, g * P : (g + 1) * P],
                            rhs=x_c[b][:, cols].bitcast(FP8X4),
                            rhs_scale=x_s[b][:, cols],
                            start=(b == 0 and e == 0),
                            stop=(b == PASSES - 1 and e == per - 1),
                        )
                for b in range(PASSES):
                    for e in range(per):
                        g = per * part + e
                        nc.tensor.matmul_mx(
                            out=base[:, e * width : (e + 1) * width],
                            lhsT=w4_c[:, b, 2 * g * P : 2 * (g + 1) * P].bitcast(FP4X4),
                            lhsT_scale=w4_s[:, b, g * P : (g + 1) * P],
                            rhs=x_c[b][:, cols].bitcast(FP8X4),
                            rhs_scale=x_s[b][:, cols],
                            start=(b == 0 and e == 0),
                            stop=(b == PASSES - 1 and e == per - 1),
                        )
                for e in range(per):
                    g = per * part + e
                    nc.scalar.activation(
                        res[:, g, :], pre[:, e * width : (e + 1) * width], ACT.Tanh, bias=bias[:, g : g + 1]
                    )
                bent = res[:, per * part : per * (part + 1), :].rearrange("p g m -> p (g m)")
                nc.vector.tensor_tensor(bent, base[:, : per * width], bent, ADD)
            nc.sync.dma_start(out_rows[:, :, cols], res[:])

        gather_early(SLICES - 1)
        quantize_x1(0)
        quantize_x0()
        for c in range(1, len(CHUNKS)):
            quantize_x1(c)
            products(c - 1)
        products(len(CHUNKS) - 1)
